import numpy as np, ml_dtypes
CORES = [2,7,10,15,18,23,26,31,34,39,42,47,50,55]
N = 14
F = 64
def setup_inputs(rng):
    return {"a": rng.standard_normal((N, 128, 128), dtype=np.float32).astype(ml_dtypes.bfloat16), "w": rng.standard_normal((N, 128, N * F), dtype=np.float32).astype(ml_dtypes.bfloat16)}
def reference(a, w):
    tot = np.zeros((128, N * F))
    for j in range(N):
        tot += a[j].astype(np.float64).T @ w[j].astype(np.float64)
    return {"y": np.stack([tot[:, F * r:F * r + F] for r in range(N)]).astype(ml_dtypes.bfloat16 if a.dtype != np.float64 else np.float64)}

@@ -1,0 +1,219 @@
+from concourse.bass import DstId, RemoteDMATransfer
+from concourse.mybir import AluOpType
+
+F = 64
+N = 14
+PER_AGENT = 4
+W1 = PER_AGENT + 1
+CHUNK = 3
+
+SCRATCH = {
+    "a_sb": ("sbuf", [128, 128], "bfloat16"),
+    "w_sb": ("sbuf", [128, N * F], "bfloat16"),
+    "s1": ("sbuf", [128, (2 * PER_AGENT + 1) * F], "bfloat16"),
+    "l1": ("sbuf", [128, 2 * W1 * F], "bfloat16"),
+    "s2": ("sbuf", [128, PER_AGENT * F], "bfloat16"),
+    "l2": ("sbuf", [128, 6 * F], "bfloat16"),
+    "y_sb": ("sbuf", [128, F], "bfloat16"),
+    "p0": ("psum", [128, 512], "float32"),
+    "p1": ("psum", [128, 512], "float32"),
+    "p2": ("psum", [128, 512], "float32"),
+    "p3": ("psum", [128, 512], "float32"),
+    "p4": ("psum", [128, 512], "float32"),
+}
+SEMAPHORES = ["ld", "m0", "m1", "m2", "m3", "m4", "cp", "l1", "ad", "ac", "yr", "st", "loc",
+              "x0", "x1", "x2", "x3", "x4", "x5"]
+
+_CACHE = {}
+
+
+def _split(mask, n):
+    bits = [b for b in range(mask.bit_length()) if (mask >> b) & 1]
+    per = 1
+    while per * 2 * n <= len(bits):
+        per *= 2
+    return [sum(1 << b for b in bits[i * per:(i + 1) * per]) for i in range(n)], per
+
+
+def _hops(topo, c, x):
+    return 1 if (topo.mates(c, x) or topo.same_plane(c, x)) else 2
+
+
+def _plan(cores, topo):
+    key = tuple(cores)
+    if key in _CACHE:
+        return _CACHE[key]
+    chips = sorted(set(topo.chip(c) for c in cores))
+    dies = sorted(set(topo.die(c) for c in cores))
+
+    def ports(c, d, x):
+        if topo.same_plane(c, x):
+            return [("out", c, d), ("in", x, d)]
+        if topo.mates(c, x):
+            return [("mate", c, d)]
+        m = [k for k in range(topo.CHIPS) if topo.mates(c, k)][0]
+        return [("mate", c, d), ("out", m, d), ("in", x, d)]
+
+    away = {c: [t for t in cores if topo.chip(t) != c] for c in chips}
+
+    def die_of(c, t, x, moved):
+        return x if (topo.die(t) == x or t in moved) else topo.die(t)
+
+    def cost(X, M):
+        load = {}
+        for c in chips:
+            for t in away[c]:
+                for p in ports(c, die_of(c, t, X[c], M[c]), topo.chip(t)):
+                    load[p] = load.get(p, 0) + 1
+        return (max(load.values()), sum(v * v for v in load.values()))
+
+    def pairs(c, x):
+        cand = [t for t in away[c] if topo.die(t) != x]
+        return [(cand[i], cand[j]) for i in range(len(cand)) for j in range(i + 1, len(cand))]
+
+    X = {c: dies[0] for c in chips}
+    M = {c: pairs(c, X[c])[0] for c in chips}
+    cur = cost(X, M)
+    better = True
+    while better:
+        better = False
+        for c in chips:
+            for x in dies:
+                for pr in pairs(c, x):
+                    X2, M2 = dict(X), dict(M)
+                    X2[c], M2[c] = x, pr
+                    k = cost(X2, M2)
+                    if k < cur:
+                        cur, X, M, better = k, X2, M2, True
+
+    plan = {}
+    for c in chips:
+        ranks = [t for t in cores if topo.chip(t) == c]
+        helper = [h for h in range(topo.CHIPS * topo.CORES_PER_CHIP)
+                  if topo.chip(h) == c and topo.die(h) == X[c] and h not in ranks
+                  and all(topo.may_write(h, t) for t in away[c])][0]
+        by_die = {d: [t for t in away[c] if die_of(c, t, X[c], M[c]) == d] for d in dies}
+        jobs = []
+        for r in ranks:
+            lot = sorted(by_die[topo.die(r)], key=lambda t: (_hops(topo, c, topo.chip(t)), t))
+            if topo.die(r) == X[c]:
+                jobs.append((helper, lot[:PER_AGENT]))
+                lot = lot[PER_AGENT:]
+            jobs.append((r, lot))
+        plan[c] = jobs
+    _CACHE[key] = plan
+    return plan
+
+
+def rank_program(g, core, T, topo):
+    cores = list(T.cores)
+    plan = _plan(cores, topo)
+    chip = topo.chip(core)
+    jobs = dict(plan.get(chip, []))
+    if core not in jobs:
+        return
+    S = T.sem
+    pe, ve = g.tensor, g.vector
+    add = AluOpType.add
+    rank = T.rank_of(core)
+    mine = jobs[core]
+    nb = len(mine)
+    here = [c for c in cores if topo.chip(c) == chip]
+    sent = 0
+
+    def blk(t, i, n=1):
+        return t[:, i * F:(i + n) * F]
+
+    def to(dst, mask, sem, src_ap, dst_ap):
+        rid, pid, _ = topo.addr(dst)
+        return RemoteDMATransfer(dst_ids=[DstId(rid=rid, pnc=pid)], dma_engine_mask=mask, remote_sem=sem,
+                                 src=src_ap, dst=dst_ap)
+
+    def slot_of(src_chip, dst_chip):
+        return [c for c in sorted(plan) if c != dst_chip].index(src_chip)
+
+    if rank is not None:
+        partner = [c for c in here if c != core][0]
+        helpers = [a for a in jobs if a not in here]
+        pieces = [(h, list(jobs[h])) for h in helpers] + [(partner, list(jobs[partner]) + [partner])]
+        order = [t for _, lot in pieces for t in lot]
+        chunks = [order[i:i + CHUNK] for i in range(0, len(order), CHUNK)]
+
+        g.sync.dma_start(T.a_sb[:], T.a[:]).then_inc(S.ld, 16)
+        g.scalar.dma_start(T.w_sb[:], T.w[:]).then_inc(S.ld, 16)
+
+        pe.wait_ge(S.ld, 32)
+
+        def mm(out, t, sem):
+            pe.matmul(out, T.a_sb[:], blk(T.w_sb, T.rank_of(t)), True, True).then_inc(sem, 1)
+
+        for q, ch in enumerate(chunks):
+            for i, t in enumerate(ch):
+                mm(blk(T["p%d" % q], i), t, S["m%d" % q])
+        for i, t in enumerate(mine):
+            mm(blk(T.p3, i), t, S.m3)
+        mm(blk(T.p4, 0), core, S.m4)
+
+        col = 0
+        for q, ch in enumerate(chunks):
+            ve.wait_ge(S["m%d" % q], len(ch))
+            ve.tensor_copy(blk(T.s1, col, len(ch)), blk(T["p%d" % q], 0, len(ch))).then_inc(S.cp, 1)
+            col += len(ch)
+
+        m1 = topo.mask(core, partner)
+        for h in helpers:
+            m1 &= topo.mask(core, h)
+        masks, per1 = _split(m1, len(pieces))
+        trs, off = [], 0
+        for (dst, lot), m in zip(pieces, masks):
+            at = 0 if dst == partner else here.index(core) * W1
+            trs.append(to(dst, m, S.l1, blk(T.s1, off, W1), blk(T.l1, at, W1)))
+            off += len(lot)
+            sent += per1
+        g.wait_ge(S.cp, len(chunks))
+        g.remote_dma_fused(trs, local_sem=S.loc)
+
+        ve.wait_ge(S.m3, nb)
+        ve.wait_ge(S.l1, per1)
+        ve.tensor_tensor(blk(T.s2, 0, nb), blk(T.p3, 0, nb), blk(T.l1, 0, nb), add).then_inc(S.ad, 1)
+    else:
+        m1 = topo.mask(here[0], core) & topo.mask(here[1], core)
+        per1 = _split(m1, 2)[1]
+        ve.wait_ge(S.l1, per1 * len(here))
+        ve.tensor_tensor(blk(T.s2, 0, nb), blk(T.l1, 0, nb), blk(T.l1, W1, nb), add).then_inc(S.ad, 1)
+
+    m2 = topo.mask(core, mine[0])
+    for t in mine:
+        m2 &= topo.mask(core, t)
+    masks, per2 = _split(m2, nb)
+    trs = []
+    for i, t in enumerate(mine):
+        k = slot_of(chip, topo.chip(t))
+        trs.append(to(t, masks[i], S["x%d" % k], blk(T.s2, i), blk(T.l2, k)))
+        sent += per2
+    g.wait_ge(S.ad, 1)
+    g.remote_dma_fused(trs, local_sem=S.loc)
+
+    if rank is not None:
+        ve.wait_ge(S.m4, 1)
+        ve.tensor_tensor(blk(T.p4, 1), blk(T.p4, 0), blk(T.l1, nb), add).then_inc(S.ac, 1)
+        others = sorted([c for c in sorted(plan) if c != chip], key=lambda c: (_hops(topo, c, chip), c))
+        for n, c in enumerate(others):
+            sender = [a for a, lot in plan[c] if core in lot][0]
+            lot = dict(plan[c])[sender]
+            m = topo.mask(sender, lot[0])
+            for t in lot:
+                m &= topo.mask(sender, t)
+            k = slot_of(c, chip)
+            ve.wait_ge(S["x%d" % k], _split(m, len(lot))[1])
+            ve.wait_ge(S.ac, n + 1)
+            src = blk(T.p4, (n + 1) % 2)
+            if n + 1 < len(others):
+                ve.tensor_tensor(blk(T.p4, n % 2), src, blk(T.l2, k), add).then_inc(S.ac, 1)
+            else:
+                ve.tensor_tensor(T.y_sb[:], src, blk(T.l2, k), add).then_inc(S.yr, 1)
+        g.sync.wait_ge(S.yr, 1)
+        g.sync.dma_start(T.y[:], T.y_sb[:]).then_inc(S.st, 16)
+        g.sync.wait_ge(S.st, 16)
+
+    g.wait_ge(S.loc, sent)

@@ -3,26 +3,21 @@ from concourse.mybir import AluOpType
 
 F = 64
 N = 14
-PER_AGENT = 4
-W1 = PER_AGENT + 1
-CHUNK = 3
+LOT = 4
+AW = 2
+W1 = AW + LOT + 1
 
 SCRATCH = {
-    "a_sb": ("sbuf", [128, 128], "bfloat16"),
-    "w_sb": ("sbuf", [128, N * F], "bfloat16"),
-    "s1": ("sbuf", [128, (2 * PER_AGENT + 1) * F], "bfloat16"),
+    "x1": ("sbuf", [128, (LOT + AW + LOT + 1) * F], "bfloat16"),
+    "wk": ("sbuf", [128, (LOT + 1) * F], "bfloat16"),
     "l1": ("sbuf", [128, 2 * W1 * F], "bfloat16"),
-    "s2": ("sbuf", [128, PER_AGENT * F], "bfloat16"),
+    "s2": ("sbuf", [128, LOT * F], "bfloat16"),
     "l2": ("sbuf", [128, 6 * F], "bfloat16"),
     "y_sb": ("sbuf", [128, F], "bfloat16"),
-    "p0": ("psum", [128, 512], "float32"),
-    "p1": ("psum", [128, 512], "float32"),
-    "p2": ("psum", [128, 512], "float32"),
     "p3": ("psum", [128, 512], "float32"),
     "p4": ("psum", [128, 512], "float32"),
 }
-SEMAPHORES = ["ld", "m0", "m1", "m2", "m3", "m4", "cp", "l1", "ad", "ac", "yr", "st", "loc",
-              "x0", "x1", "x2", "x3", "x4", "x5"]
+SEMAPHORES = ["ld", "lk", "h0", "h1", "m3", "ad", "ac", "yr", "st", "loc", "x0", "x1", "x2", "x3", "x4", "x5"]
 
 _CACHE = {}
 
@@ -54,53 +49,30 @@ def _plan(cores, topo):
         m = [k for k in range(topo.CHIPS) if topo.mates(c, k)][0]
         return [("mate", c, d), ("out", m, d), ("in", x, d)]
 
-    away = {c: [t for t in cores if topo.chip(t) != c] for c in chips}
+    first = {c: min(i for i, t in enumerate(cores) if topo.chip(t) == c) for c in chips}
+    start = {c: ((first[c] - LOT) % N, (first[c] + 2) % N, (first[c] + 2 + LOT) % N) for c in chips}
 
-    def die_of(c, t, x, moved):
-        return x if (topo.die(t) == x or t in moved) else topo.die(t)
-
-    def cost(X, M):
+    def cost(pick):
         load = {}
-        for c in chips:
-            for t in away[c]:
-                for p in ports(c, die_of(c, t, X[c], M[c]), topo.chip(t)):
-                    load[p] = load.get(p, 0) + 1
+        for c, x in zip(chips, pick):
+            for d, s in zip((topo.die(cores[first[c]]), topo.die(cores[first[c] + 1]), x), start[c]):
+                for i in range(LOT):
+                    for p in ports(c, d, topo.chip(cores[(s + i) % N])):
+                        load[p] = load.get(p, 0) + 1
         return (max(load.values()), sum(v * v for v in load.values()))
 
-    def pairs(c, x):
-        cand = [t for t in away[c] if topo.die(t) != x]
-        return [(cand[i], cand[j]) for i in range(len(cand)) for j in range(i + 1, len(cand))]
-
-    X = {c: dies[0] for c in chips}
-    M = {c: pairs(c, X[c])[0] for c in chips}
-    cur = cost(X, M)
-    better = True
-    while better:
-        better = False
-        for c in chips:
-            for x in dies:
-                for pr in pairs(c, x):
-                    X2, M2 = dict(X), dict(M)
-                    X2[c], M2[c] = x, pr
-                    k = cost(X2, M2)
-                    if k < cur:
-                        cur, X, M, better = k, X2, M2, True
+    picks = [()]
+    for c in chips:
+        picks = [p + (d,) for p in picks for d in dies]
+    pick = min(picks, key=lambda p: (cost(p), p))
 
     plan = {}
-    for c in chips:
-        ranks = [t for t in cores if topo.chip(t) == c]
+    for c, x in zip(chips, pick):
+        lot = [cores[(start[c][2] + i) % N] for i in range(LOT)]
         helper = [h for h in range(topo.CHIPS * topo.CORES_PER_CHIP)
-                  if topo.chip(h) == c and topo.die(h) == X[c] and h not in ranks
-                  and all(topo.may_write(h, t) for t in away[c])][0]
-        by_die = {d: [t for t in away[c] if die_of(c, t, X[c], M[c]) == d] for d in dies}
-        jobs = []
-        for r in ranks:
-            lot = sorted(by_die[topo.die(r)], key=lambda t: (_hops(topo, c, topo.chip(t)), t))
-            if topo.die(r) == X[c]:
-                jobs.append((helper, lot[:PER_AGENT]))
-                lot = lot[PER_AGENT:]
-            jobs.append((r, lot))
-        plan[c] = jobs
+                  if topo.chip(h) == c and topo.die(h) == x and h not in cores
+                  and all(topo.may_write(h, t) for t in lot)][0]
+        plan[c] = list(zip((cores[first[c]], cores[first[c] + 1], helper), start[c]))
     _CACHE[key] = plan
     return plan
 
@@ -116,9 +88,8 @@ def rank_program(g, core, T, topo):
     pe, ve = g.tensor, g.vector
     add = AluOpType.add
     rank = T.rank_of(core)
-    mine = jobs[core]
-    nb = len(mine)
-    here = [c for c in cores if topo.chip(c) == chip]
+    mine = [cores[(jobs[core] + i) % N] for i in range(LOT)]
+    r_first, r_second, helper = [a for a, _ in plan[chip]]
     sent = 0
 
     def blk(t, i, n=1):
@@ -132,84 +103,77 @@ def rank_program(g, core, T, topo):
     def slot_of(src_chip, dst_chip):
         return [c for c in sorted(plan) if c != dst_chip].index(src_chip)
 
+    def load_w(q, dst, at, s, n, sem):
+        k = min(n, N - s)
+        q.dma_start(blk(dst, at, k), blk(T.w, s, k)).then_inc(sem, 16)
+        if k < n:
+            q.dma_start(blk(dst, at + k, n - k), blk(T.w, 0, n - k)).then_inc(sem, 16)
+            return 32
+        return 16
+
+    masks1, per1 = _split(topo.mask(r_first, r_second) & topo.mask(r_first, helper) & topo.mask(r_second, helper), 2)
+
     if rank is not None:
-        partner = [c for c in here if c != core][0]
-        helpers = [a for a in jobs if a not in here]
-        pieces = [(h, list(jobs[h])) for h in helpers] + [(partner, list(jobs[partner]) + [partner])]
-        order = [t for _, lot in pieces for t in lot]
-        chunks = [order[i:i + CHUNK] for i in range(0, len(order), CHUNK)]
+        is_first = core == r_first
+        partner = r_second if is_first else r_first
+        run_of = {r_first: jobs[r_first], r_second: (jobs[r_second] - 1) % N}
+        own_at, lot_at = (LOT, 0) if is_first else (0, 1)
+        a_sb = blk(T.x1, LOT, AW)
 
-        g.sync.dma_start(T.a_sb[:], T.a[:]).then_inc(S.ld, 16)
-        g.scalar.dma_start(T.w_sb[:], T.w[:]).then_inc(S.ld, 16)
+        n_ld = 16
+        g.sync.dma_start(a_sb, T.a[:]).then_inc(S.ld, 16)
+        n_ld += load_w(g.scalar, T.x1, LOT + AW, run_of[partner], LOT + 1, S.ld)
+        n_ld += load_w(g.sync, T.x1, 0, jobs[helper], LOT, S.ld)
+        n_lk = load_w(g.scalar, T.wk, 0, run_of[core], LOT + 1, S.lk)
 
-        pe.wait_ge(S.ld, 32)
+        g.wait_ge(S.ld, n_ld)
+        g.remote_dma_fused([
+            to(helper, masks1[0], S.h0 if is_first else S.h1, blk(T.x1, 0, W1), blk(T.l1, 0 if is_first else W1, W1)),
+            to(partner, masks1[1], S.h0, blk(T.x1, LOT, W1), blk(T.l1, 0, W1)),
+        ], local_sem=S.loc)
+        sent += 2 * per1
 
-        def mm(out, t, sem):
-            pe.matmul(out, T.a_sb[:], blk(T.w_sb, T.rank_of(t)), True, True).then_inc(sem, 1)
-
-        for q, ch in enumerate(chunks):
-            for i, t in enumerate(ch):
-                mm(blk(T["p%d" % q], i), t, S["m%d" % q])
-        for i, t in enumerate(mine):
-            mm(blk(T.p3, i), t, S.m3)
-        mm(blk(T.p4, 0), core, S.m4)
-
-        col = 0
-        for q, ch in enumerate(chunks):
-            ve.wait_ge(S["m%d" % q], len(ch))
-            ve.tensor_copy(blk(T.s1, col, len(ch)), blk(T["p%d" % q], 0, len(ch))).then_inc(S.cp, 1)
-            col += len(ch)
-
-        m1 = topo.mask(core, partner)
-        for h in helpers:
-            m1 &= topo.mask(core, h)
-        masks, per1 = _split(m1, len(pieces))
-        trs, off = [], 0
-        for (dst, lot), m in zip(pieces, masks):
-            at = 0 if dst == partner else here.index(core) * W1
-            trs.append(to(dst, m, S.l1, blk(T.s1, off, W1), blk(T.l1, at, W1)))
-            off += len(lot)
-            sent += per1
-        g.wait_ge(S.cp, len(chunks))
-        g.remote_dma_fused(trs, local_sem=S.loc)
-
-        ve.wait_ge(S.m3, nb)
-        ve.wait_ge(S.l1, per1)
-        ve.tensor_tensor(blk(T.s2, 0, nb), blk(T.p3, 0, nb), blk(T.l1, 0, nb), add).then_inc(S.ad, 1)
+        pe.wait_ge(S.ld, n_ld)
+        pe.wait_ge(S.lk, n_lk)
+        pe.matmul(blk(T.p3, 0, LOT + 1), a_sb, T.wk[:], True, False).then_inc(S.m3, 1)
+        pe.wait_ge(S.h0, per1)
+        pe.matmul(blk(T.p3, 0, LOT + 1), blk(T.l1, 0, AW), blk(T.l1, AW, LOT + 1), False, True).then_inc(S.m3, 1)
     else:
-        m1 = topo.mask(here[0], core) & topo.mask(here[1], core)
-        per1 = _split(m1, 2)[1]
-        ve.wait_ge(S.l1, per1 * len(here))
-        ve.tensor_tensor(blk(T.s2, 0, nb), blk(T.l1, 0, nb), blk(T.l1, W1, nb), add).then_inc(S.ad, 1)
+        lot_at = 0
+        pe.wait_ge(S.h0, per1)
+        pe.matmul(blk(T.p3, 0, LOT), blk(T.l1, LOT, AW), blk(T.l1, 0, LOT), True, False).then_inc(S.m3, 1)
+        pe.wait_ge(S.h1, per1)
+        pe.matmul(blk(T.p3, 0, LOT), blk(T.l1, W1 + LOT, AW), blk(T.l1, W1, LOT), False, True).then_inc(S.m3, 1)
 
-    m2 = topo.mask(core, mine[0])
-    for t in mine:
-        m2 &= topo.mask(core, t)
-    masks, per2 = _split(m2, nb)
+    ve.wait_ge(S.m3, 2)
+    ve.tensor_copy(T.s2[:], blk(T.p3, lot_at, LOT)).then_inc(S.ad, 1)
+
+    def engines(src, lot):
+        m = topo.mask(src, lot[0])
+        for t in lot:
+            m &= topo.mask(src, t)
+        return _split(m, len(lot))
+
+    masks2, per2 = engines(core, mine)
     trs = []
     for i, t in enumerate(mine):
         k = slot_of(chip, topo.chip(t))
-        trs.append(to(t, masks[i], S["x%d" % k], blk(T.s2, i), blk(T.l2, k)))
+        trs.append(to(t, masks2[i], S["x%d" % k], blk(T.s2, i), blk(T.l2, k)))
         sent += per2
     g.wait_ge(S.ad, 1)
     g.remote_dma_fused(trs, local_sem=S.loc)
 
     if rank is not None:
-        ve.wait_ge(S.m4, 1)
-        ve.tensor_tensor(blk(T.p4, 1), blk(T.p4, 0), blk(T.l1, nb), add).then_inc(S.ac, 1)
         others = sorted([c for c in sorted(plan) if c != chip], key=lambda c: (_hops(topo, c, chip), c))
         for n, c in enumerate(others):
-            sender = [a for a, lot in plan[c] if core in lot][0]
-            lot = dict(plan[c])[sender]
-            m = topo.mask(sender, lot[0])
-            for t in lot:
-                m &= topo.mask(sender, t)
+            sender, s = [(a, s) for a, s in plan[c] if (rank - s) % N < LOT][0]
             k = slot_of(c, chip)
-            ve.wait_ge(S["x%d" % k], _split(m, len(lot))[1])
-            ve.wait_ge(S.ac, n + 1)
-            src = blk(T.p4, (n + 1) % 2)
+            ve.wait_ge(S["x%d" % k], engines(sender, [cores[(s + i) % N] for i in range(LOT)])[1])
+            if n:
+                ve.wait_ge(S.ac, n)
+            src = blk(T.p4, n % 2) if n else blk(T.p3, own_at)
             if n + 1 < len(others):
-                ve.tensor_tensor(blk(T.p4, n % 2), src, blk(T.l2, k), add).then_inc(S.ac, 1)
+                ve.tensor_tensor(blk(T.p4, (n + 1) % 2), src, blk(T.l2, k), add).then_inc(S.ac, 1)
             else:
                 ve.tensor_tensor(T.y_sb[:], src, blk(T.l2, k), add).then_inc(S.yr, 1)
         g.sync.wait_ge(S.yr, 1)

@@ -3,23 +3,30 @@ from concourse.mybir import AluOpType
 
 F = 64
 N = 14
-LOT = 4
+LOT = 2
 AW = 2
-W1 = AW + LOT + 1
+RL = LOT + 1
+W1 = AW + RL
+ND = N - 2 - 3 * LOT
+DA = 4
+NS = 3 + 2 * (ND // 2)
 
 SCRATCH = {
-    "x1": ("sbuf", [128, (LOT + AW + LOT + 1) * F], "bfloat16"),
-    "wk": ("sbuf", [128, (LOT + 1) * F], "bfloat16"),
+    "x1": ("sbuf", [128, (LOT + AW + RL) * F], "bfloat16"),
+    "wk": ("sbuf", [128, RL * F], "bfloat16"),
+    "wd": ("sbuf", [128, ND * F], "bfloat16"),
+    "sd": ("sbuf", [128, ND * F], "bfloat16"),
     "l1": ("sbuf", [128, 2 * W1 * F], "bfloat16"),
     "s2": ("sbuf", [128, LOT * F], "bfloat16"),
-    "l2": ("sbuf", [128, 6 * F], "bfloat16"),
+    "l2": ("sbuf", [128, NS * F], "bfloat16"),
     "y_sb": ("sbuf", [128, F], "bfloat16"),
+    "p0": ("psum", [128, 512], "float32"),
+    "p1": ("psum", [128, 512], "float32"),
     "p3": ("psum", [128, 512], "float32"),
     "p4": ("psum", [128, 512], "float32"),
 }
-SEMAPHORES = ["ld", "lk", "h0", "h1", "m3", "ad", "ac", "yr", "st", "loc", "x0", "x1", "x2", "x3", "x4", "x5"]
-
-_CACHE = {}
+SEMAPHORES = ["ld", "lk", "lw", "h0", "h1", "m0", "m1", "m3", "c0", "c1", "ad", "ac", "yr", "st", "loc"] + \
+             ["x%d" % i for i in range(NS)]
 
 
 def _split(mask, n):
@@ -30,66 +37,30 @@ def _split(mask, n):
     return [sum(1 << b for b in bits[i * per:(i + 1) * per]) for i in range(n)], per
 
 
-def _hops(topo, c, x):
-    return 1 if (topo.mates(c, x) or topo.same_plane(c, x)) else 2
-
-
-def _plan(cores, topo):
-    key = tuple(cores)
-    if key in _CACHE:
-        return _CACHE[key]
-    chips = sorted(set(topo.chip(c) for c in cores))
-    dies = sorted(set(topo.die(c) for c in cores))
-
-    def ports(c, d, x):
-        if topo.same_plane(c, x):
-            return [("out", c, d), ("in", x, d)]
-        if topo.mates(c, x):
-            return [("mate", c, d)]
-        m = [k for k in range(topo.CHIPS) if topo.mates(c, k)][0]
-        return [("mate", c, d), ("out", m, d), ("in", x, d)]
-
-    first = {c: min(i for i, t in enumerate(cores) if topo.chip(t) == c) for c in chips}
-    start = {c: ((first[c] - LOT) % N, (first[c] + 2) % N, (first[c] + 2 + LOT) % N) for c in chips}
-
-    def cost(pick):
-        load = {}
-        for c, x in zip(chips, pick):
-            for d, s in zip((topo.die(cores[first[c]]), topo.die(cores[first[c] + 1]), x), start[c]):
-                for i in range(LOT):
-                    for p in ports(c, d, topo.chip(cores[(s + i) % N])):
-                        load[p] = load.get(p, 0) + 1
-        return (max(load.values()), sum(v * v for v in load.values()))
-
-    picks = [()]
-    for c in chips:
-        picks = [p + (d,) for p in picks for d in dies]
-    pick = min(picks, key=lambda p: (cost(p), p))
-
-    plan = {}
-    for c, x in zip(chips, pick):
-        lot = [cores[(start[c][2] + i) % N] for i in range(LOT)]
-        helper = [h for h in range(topo.CHIPS * topo.CORES_PER_CHIP)
-                  if topo.chip(h) == c and topo.die(h) == x and h not in cores
-                  and all(topo.may_write(h, t) for t in lot)][0]
-        plan[c] = list(zip((cores[first[c]], cores[first[c] + 1], helper), start[c]))
-    _CACHE[key] = plan
-    return plan
-
-
 def rank_program(g, core, T, topo):
     cores = list(T.cores)
-    plan = _plan(cores, topo)
     chip = topo.chip(core)
-    jobs = dict(plan.get(chip, []))
-    if core not in jobs:
+    here = [c for c in cores if topo.chip(c) == chip]
+    if not here:
+        return
+    r_first, r_second = here
+    f = T.rank_of(r_first)
+    REL = {"first": N - LOT, "second": 2, "helper": 2 + LOT, "direct": 2 + 2 * LOT}
+
+    def ring(rel, n):
+        return [cores[(f + rel + i) % N] for i in range(n)]
+
+    helper = [h for h in range(topo.CHIPS * topo.CORES_PER_CHIP)
+              if topo.chip(h) == chip and h not in cores
+              and all(topo.may_write(h, t) for t in ring(REL["helper"], LOT))][0]
+    if core not in (r_first, r_second, helper):
         return
     S = T.sem
     pe, ve = g.tensor, g.vector
     add = AluOpType.add
     rank = T.rank_of(core)
-    mine = [cores[(jobs[core] + i) % N] for i in range(LOT)]
-    r_first, r_second, helper = [a for a, _ in plan[chip]]
+    role = "first" if core == r_first else "second" if core == r_second else "helper"
+    mine = ring(REL[role], LOT)
     sent = 0
 
     def blk(t, i, n=1):
@@ -100,10 +71,23 @@ def rank_program(g, core, T, topo):
         return RemoteDMATransfer(dst_ids=[DstId(rid=rid, pnc=pid)], dma_engine_mask=mask, remote_sem=sem,
                                  src=src_ap, dst=dst_ap)
 
-    def slot_of(src_chip, dst_chip):
-        return [c for c in sorted(plan) if c != dst_chip].index(src_chip)
+    def slot_of(rel, second):
+        if rel >= REL["first"]:
+            return 0
+        if rel < REL["helper"]:
+            return 1
+        if rel < REL["direct"]:
+            return 2
+        return 3 + 2 * ((rel - REL["direct"]) // 2) + (1 if second else 0)
 
-    def load_w(q, dst, at, s, n, sem):
+    def off_chip(src, lot):
+        m = topo.mask(src, lot[0])
+        for t in lot:
+            m &= topo.mask(src, t)
+        return _split(m, len(lot))
+
+    def load_w(q, dst, at, rel, n, sem):
+        s = (f + rel) % N
         k = min(n, N - s)
         q.dma_start(blk(dst, at, k), blk(T.w, s, k)).then_inc(sem, 16)
         if k < n:
@@ -114,17 +98,18 @@ def rank_program(g, core, T, topo):
     masks1, per1 = _split(topo.mask(r_first, r_second) & topo.mask(r_first, helper) & topo.mask(r_second, helper), 2)
 
     if rank is not None:
-        is_first = core == r_first
+        is_first = role == "first"
         partner = r_second if is_first else r_first
-        run_of = {r_first: jobs[r_first], r_second: (jobs[r_second] - 1) % N}
+        run_rel = {"first": REL["first"], "second": 1}
         own_at, lot_at = (LOT, 0) if is_first else (0, 1)
         a_sb = blk(T.x1, LOT, AW)
 
         n_ld = 16
         g.sync.dma_start(a_sb, T.a[:]).then_inc(S.ld, 16)
-        n_ld += load_w(g.scalar, T.x1, LOT + AW, run_of[partner], LOT + 1, S.ld)
-        n_ld += load_w(g.sync, T.x1, 0, jobs[helper], LOT, S.ld)
-        n_lk = load_w(g.scalar, T.wk, 0, run_of[core], LOT + 1, S.lk)
+        n_ld += load_w(g.scalar, T.x1, LOT + AW, run_rel["second" if is_first else "first"], RL, S.ld)
+        n_ld += load_w(g.sync, T.x1, 0, REL["helper"], LOT, S.ld)
+        n_lw = load_w(g.scalar, T.wd, 0, REL["direct"], ND, S.lw)
+        n_lk = load_w(g.sync, T.wk, 0, run_rel[role], RL, S.lk)
 
         g.wait_ge(S.ld, n_ld)
         g.remote_dma_fused([
@@ -134,10 +119,26 @@ def rank_program(g, core, T, topo):
         sent += 2 * per1
 
         pe.wait_ge(S.ld, n_ld)
+        pe.wait_ge(S.lw, n_lw)
+        pe.matmul(blk(T.p0, 0, DA), a_sb, blk(T.wd, 0, DA), True, True).then_inc(S.m0, 1)
+        pe.matmul(blk(T.p1, 0, ND - DA), a_sb, blk(T.wd, DA, ND - DA), True, True).then_inc(S.m1, 1)
+        direct = ring(REL["direct"], ND)
+        for lo, n, ps, ms, cs in ((0, DA, T.p0, S.m0, S.c0), (DA, ND - DA, T.p1, S.m1, S.c1)):
+            ve.wait_ge(ms, 1)
+            ve.tensor_copy(blk(T.sd, lo, n), blk(ps, 0, n)).then_inc(cs, 1)
+            masks, per = off_chip(core, direct[lo:lo + n])
+            trs = []
+            for i in range(n):
+                k = slot_of(REL["direct"] + lo + i, not is_first)
+                trs.append(to(direct[lo + i], masks[i], S["x%d" % k], blk(T.sd, lo + i), blk(T.l2, k)))
+                sent += per
+            g.wait_ge(cs, 1)
+            g.remote_dma_fused(trs, local_sem=S.loc)
+
         pe.wait_ge(S.lk, n_lk)
-        pe.matmul(blk(T.p3, 0, LOT + 1), a_sb, T.wk[:], True, False).then_inc(S.m3, 1)
+        pe.matmul(blk(T.p3, 0, RL), a_sb, T.wk[:], True, False).then_inc(S.m3, 1)
         pe.wait_ge(S.h0, per1)
-        pe.matmul(blk(T.p3, 0, LOT + 1), blk(T.l1, 0, AW), blk(T.l1, AW, LOT + 1), False, True).then_inc(S.m3, 1)
+        pe.matmul(blk(T.p3, 0, RL), blk(T.l1, 0, AW), blk(T.l1, AW, RL), False, True).then_inc(S.m3, 1)
     else:
         lot_at = 0
         pe.wait_ge(S.h0, per1)
@@ -148,31 +149,25 @@ def rank_program(g, core, T, topo):
     ve.wait_ge(S.m3, 2)
     ve.tensor_copy(T.s2[:], blk(T.p3, lot_at, LOT)).then_inc(S.ad, 1)
 
-    def engines(src, lot):
-        m = topo.mask(src, lot[0])
-        for t in lot:
-            m &= topo.mask(src, t)
-        return _split(m, len(lot))
-
-    masks2, per2 = engines(core, mine)
+    masks2, per2 = off_chip(core, mine)
     trs = []
     for i, t in enumerate(mine):
-        k = slot_of(chip, topo.chip(t))
+        k = slot_of(REL[role] + i, False)
         trs.append(to(t, masks2[i], S["x%d" % k], blk(T.s2, i), blk(T.l2, k)))
         sent += per2
     g.wait_ge(S.ad, 1)
     g.remote_dma_fused(trs, local_sem=S.loc)
 
     if rank is not None:
-        others = sorted([c for c in sorted(plan) if c != chip], key=lambda c: (_hops(topo, c, chip), c))
-        for n, c in enumerate(others):
-            sender, s = [(a, s) for a, s in plan[c] if (rank - s) % N < LOT][0]
-            k = slot_of(c, chip)
-            ve.wait_ge(S["x%d" % k], engines(sender, [cores[(s + i) % N] for i in range(LOT)])[1])
+        per_a = off_chip(core, direct[:DA])[1]
+        per_b = off_chip(core, direct[DA:])[1]
+        order = [(k, per_a if (k - 3) < DA else per_b) for k in range(3, NS)] + [(k, per2) for k in range(3)]
+        for n, (k, per) in enumerate(order):
+            ve.wait_ge(S["x%d" % k], per)
             if n:
                 ve.wait_ge(S.ac, n)
             src = blk(T.p4, n % 2) if n else blk(T.p3, own_at)
-            if n + 1 < len(others):
+            if n + 1 < len(order):
                 ve.tensor_tensor(blk(T.p4, (n + 1) % 2), src, blk(T.l2, k), add).then_inc(S.ac, 1)
             else:
                 ve.tensor_tensor(T.y_sb[:], src, blk(T.l2, k), add).then_inc(S.yr, 1)

from concourse.bass import DstId, RemoteDMATransfer
from concourse.mybir import AluOpType

F = 64
N = 14
LOT = 2
AW = 2
RL = LOT + 1
W1 = AW + RL
ND = N - 2 - 3 * LOT
DA = 4
NS = 3 + 2 * (ND // 2)

SCRATCH = {
    "x1": ("sbuf", [128, (LOT + AW + RL) * F], "bfloat16"),
    "wk": ("sbuf", [128, RL * F], "bfloat16"),
    "wd": ("sbuf", [128, ND * F], "bfloat16"),
    "sd": ("sbuf", [128, ND * F], "bfloat16"),
    "l1": ("sbuf", [128, 2 * W1 * F], "bfloat16"),
    "s2": ("sbuf", [128, LOT * F], "bfloat16"),
    "l2": ("sbuf", [128, NS * F], "bfloat16"),
    "y_sb": ("sbuf", [128, F], "bfloat16"),
    "p0": ("psum", [128, 512], "float32"),
    "p1": ("psum", [128, 512], "float32"),
    "p3": ("psum", [128, 512], "float32"),
    "p4": ("psum", [128, 512], "float32"),
}
SEMAPHORES = ["ld", "lk", "lw", "h0", "h1", "m0", "m1", "m3", "c0", "c1", "ad", "ac", "yr", "st", "loc"] + \
             ["x%d" % i for i in range(NS)]


def _split(mask, n):
    bits = [b for b in range(mask.bit_length()) if (mask >> b) & 1]
    per = 1
    while per * 2 * n <= len(bits):
        per *= 2
    return [sum(1 << b for b in bits[i * per:(i + 1) * per]) for i in range(n)], per


def rank_program(g, core, T, topo):
    cores = list(T.cores)
    chip = topo.chip(core)
    here = [c for c in cores if topo.chip(c) == chip]
    if not here:
        return
    r_first, r_second = here
    f = T.rank_of(r_first)
    REL = {"first": N - LOT, "second": 2, "helper": 2 + LOT, "direct": 2 + 2 * LOT}

    def ring(rel, n):
        return [cores[(f + rel + i) % N] for i in range(n)]

    helper = [h for h in range(topo.CHIPS * topo.CORES_PER_CHIP)
              if topo.chip(h) == chip and h not in cores
              and all(topo.may_write(h, t) for t in ring(REL["helper"], LOT))][0]
    if core not in (r_first, r_second, helper):
        return
    S = T.sem
    pe, ve = g.tensor, g.vector
    add = AluOpType.add
    rank = T.rank_of(core)
    role = "first" if core == r_first else "second" if core == r_second else "helper"
    mine = ring(REL[role], LOT)
    sent = 0

    def blk(t, i, n=1):
        return t[:, i * F:(i + n) * F]

    def to(dst, mask, sem, src_ap, dst_ap):
        rid, pid, _ = topo.addr(dst)
        return RemoteDMATransfer(dst_ids=[DstId(rid=rid, pnc=pid)], dma_engine_mask=mask, remote_sem=sem,
                                 src=src_ap, dst=dst_ap)

    def slot_of(rel, second):
        if rel >= REL["first"]:
            return 0
        if rel < REL["helper"]:
            return 1
        if rel < REL["direct"]:
            return 2
        return 3 + 2 * ((rel - REL["direct"]) // 2) + (1 if second else 0)

    def off_chip(src, lot):
        m = topo.mask(src, lot[0])
        for t in lot:
            m &= topo.mask(src, t)
        return _split(m, len(lot))

    def load_w(q, dst, at, rel, n, sem):
        s = (f + rel) % N
        k = min(n, N - s)
        q.dma_start(blk(dst, at, k), blk(T.w, s, k)).then_inc(sem, 16)
        if k < n:
            q.dma_start(blk(dst, at + k, n - k), blk(T.w, 0, n - k)).then_inc(sem, 16)
            return 32
        return 16

    masks1, per1 = _split(topo.mask(r_first, r_second) & topo.mask(r_first, helper) & topo.mask(r_second, helper), 2)

    if rank is not None:
        is_first = role == "first"
        partner = r_second if is_first else r_first
        run_rel = {"first": REL["first"], "second": 1}
        own_at, lot_at = (LOT, 0) if is_first else (0, 1)
        a_sb = blk(T.x1, LOT, AW)

        n_ld = 16
        g.sync.dma_start(a_sb, T.a[:]).then_inc(S.ld, 16)
        n_ld += load_w(g.scalar, T.x1, LOT + AW, run_rel["second" if is_first else "first"], RL, S.ld)
        n_ld += load_w(g.sync, T.x1, 0, REL["helper"], LOT, S.ld)
        n_lw = load_w(g.scalar, T.wd, 0, REL["direct"], ND, S.lw)
        n_lk = load_w(g.sync, T.wk, 0, run_rel[role], RL, S.lk)

        g.wait_ge(S.ld, n_ld)
        g.remote_dma_fused([
            to(helper, masks1[0], S.h0 if is_first else S.h1, blk(T.x1, 0, W1), blk(T.l1, 0 if is_first else W1, W1)),
            to(partner, masks1[1], S.h0, blk(T.x1, LOT, W1), blk(T.l1, 0, W1)),
        ], local_sem=S.loc)
        sent += 2 * per1

        pe.wait_ge(S.ld, n_ld)
        pe.wait_ge(S.lw, n_lw)
        pe.matmul(blk(T.p0, 0, DA), a_sb, blk(T.wd, 0, DA), True, True).then_inc(S.m0, 1)
        pe.matmul(blk(T.p1, 0, ND - DA), a_sb, blk(T.wd, DA, ND - DA), True, True).then_inc(S.m1, 1)
        direct = ring(REL["direct"], ND)
        for lo, n, ps, ms, cs in ((0, DA, T.p0, S.m0, S.c0), (DA, ND - DA, T.p1, S.m1, S.c1)):
            ve.wait_ge(ms, 1)
            ve.tensor_copy(blk(T.sd, lo, n), blk(ps, 0, n)).then_inc(cs, 1)
            masks, per = off_chip(core, direct[lo:lo + n])
            trs = []
            for i in range(n):
                k = slot_of(REL["direct"] + lo + i, not is_first)
                trs.append(to(direct[lo + i], masks[i], S["x%d" % k], blk(T.sd, lo + i), blk(T.l2, k)))
                sent += per
            g.wait_ge(cs, 1)
            g.remote_dma_fused(trs, local_sem=S.loc)

        pe.wait_ge(S.lk, n_lk)
        pe.matmul(blk(T.p3, 0, RL), a_sb, T.wk[:], True, False).then_inc(S.m3, 1)
        pe.wait_ge(S.h0, per1)
        pe.matmul(blk(T.p3, 0, RL), blk(T.l1, 0, AW), blk(T.l1, AW, RL), False, True).then_inc(S.m3, 1)
    else:
        lot_at = 0
        pe.wait_ge(S.h0, per1)
        pe.matmul(blk(T.p3, 0, LOT), blk(T.l1, LOT, AW), blk(T.l1, 0, LOT), True, False).then_inc(S.m3, 1)
        pe.wait_ge(S.h1, per1)
        pe.matmul(blk(T.p3, 0, LOT), blk(T.l1, W1 + LOT, AW), blk(T.l1, W1, LOT), False, True).then_inc(S.m3, 1)

    ve.wait_ge(S.m3, 2)
    ve.tensor_copy(T.s2[:], blk(T.p3, lot_at, LOT)).then_inc(S.ad, 1)

    masks2, per2 = off_chip(core, mine)
    trs = []
    for i, t in enumerate(mine):
        k = slot_of(REL[role] + i, False)
        trs.append(to(t, masks2[i], S["x%d" % k], blk(T.s2, i), blk(T.l2, k)))
        sent += per2
    g.wait_ge(S.ad, 1)
    g.remote_dma_fused(trs, local_sem=S.loc)

    if rank is not None:
        per_a = off_chip(core, direct[:DA])[1]
        per_b = off_chip(core, direct[DA:])[1]
        order = [(k, per_a if (k - 3) < DA else per_b) for k in range(3, NS)] + [(k, per2) for k in range(3)]
        for n, (k, per) in enumerate(order):
            ve.wait_ge(S["x%d" % k], per)
            if n:
                ve.wait_ge(S.ac, n)
            src = blk(T.p4, n % 2) if n else blk(T.p3, own_at)
            if n + 1 < len(order):
                ve.tensor_tensor(blk(T.p4, (n + 1) % 2), src, blk(T.l2, k), add).then_inc(S.ac, 1)
            else:
                ve.tensor_tensor(T.y_sb[:], src, blk(T.l2, k), add).then_inc(S.yr, 1)
        g.sync.wait_ge(S.yr, 1)
        g.sync.dma_start(T.y[:], T.y_sb[:]).then_inc(S.st, 16)
        g.sync.wait_ge(S.st, 16)

    g.wait_ge(S.loc, sent)
